import numpy as np
import ml_dtypes


def mxq(x, axis, fmt="e4m3"):
    dtype, down = {"e4m3": (ml_dtypes.float8_e4m3fn, 7), "e5m2": (ml_dtypes.float8_e5m2, 14)}[fmt]
    v = np.moveaxis(np.asarray(x, np.float32).astype(ml_dtypes.bfloat16).astype(np.float64), axis, -1)
    blocks = v.reshape(v.shape[:-1] + (-1, 32))
    amax = np.abs(blocks).max(-1, keepdims=True)
    byte = np.maximum(np.where(amax > 0, np.frexp(amax)[1] - 1 + 127, 0) - down, 1)
    scale = np.exp2(byte - 127.0)
    codes = (blocks / scale).astype(np.float32).astype(dtype).astype(np.float64)
    return np.moveaxis((codes * scale).reshape(v.shape), -1, axis)


WIDE = False


def mx_kscale(k):
    if not WIDE:
        return np.ones(k)
    levels = np.array([10, -10, 5, -5, 0])
    if k % 512:
        return np.exp2(np.random.permutation(np.resize(levels, k // 32))).repeat(32)
    a = np.empty((k // 512, 16))
    for p in range(k // 512):
        a[p, :8] = np.random.permutation(np.resize(levels, 8))
        for g in range(8):
            far = levels[np.abs(levels - a[p, g]) >= 10]
            a[p, g + 8] = far[np.random.randint(len(far))]
    return np.exp2(a.ravel()).repeat(32)


def f64(x):
    return np.asarray(x).astype(np.float64)


def striped(idx):
    return np.tile(idx.reshape(-1, 16).T, (8, 1)).astype(np.uint16)


def unstriped(offs):
    return offs[:16].T.reshape(-1).astype(np.int64)


def pack_weight(w):
    k, n = w.shape
    w = f64(np.asarray(w, np.float32).astype(ml_dtypes.bfloat16)).reshape(k // 32, 32, n)
    amax = np.abs(w).max(1)
    byte = np.clip(np.where(amax > 0, np.frexp(amax)[1] - 1 + 127 - 7, 1), 1, 254)
    scaled = (w * np.exp2(127.0 - byte)[:, None, :]).reshape(k, n).astype(np.float32)
    words = np.ascontiguousarray(scaled.reshape(k // 512, 128, 4, n).transpose(0, 1, 3, 2)).astype(ml_dtypes.float8_e4m3fn).view(np.uint8)
    return words, np.ascontiguousarray(byte.astype(np.uint8).reshape(k // 512, 16, n))


def unpack_weight(words, scales):
    g, p, n, _ = words.shape
    vals = np.ascontiguousarray(words).view(ml_dtypes.float8_e4m3fn).astype(np.float64) * np.repeat(np.exp2(scales.astype(np.float64) - 127.0), 8, axis=1)[..., None]
    return vals.transpose(0, 1, 3, 2).reshape(g * 512, n)


K, T, S, N, H = 512, 1024, 512, 256, 512


def setup_inputs():
    n = np.random.standard_normal
    s = mx_kscale(K)[:, None]
    u = mx_kscale(H)
    packed_xT = pack_weight(n((K, T)) * s)
    return {
        "x_words": packed_xT[0],
        "x_scales": packed_xT[1],
        "w1": (n((K, H)) / np.sqrt(K) / s).astype(np.float32),
        "w2": (n((K, H)) / np.sqrt(K) / s).astype(np.float32),
        "eps": (np.random.uniform(0.3, 0.9, (H, 1))).astype(np.float32),
        "unit": (np.random.uniform(0.6, 1.4, (H, 1)) * u[:, None]).astype(np.float32),
        "w3": (n((H, N)) / np.sqrt(H) / u[:, None]).astype(np.float32),
        "offs": striped(np.random.permutation(T)[:S]),
        "lft": striped(np.random.permutation(S)),
        "rgt": striped(np.random.permutation(S)),
    }


def reference(x_words, x_scales, w1, w2, eps, unit, w3, offs, lft, rgt):
    xq = unpack_weight(x_words, x_scales)[:, unstriped(offs)]
    vv = mxq(f64(w1), 0, "e4m3").T @ xq
    vb = np.tanh(vv)
    ww = mxq(f64(w2), 0, "e4m3").T @ xq
    vl = vb[:, unstriped(lft)]
    vr = vb[:, unstriped(rgt)]
    lap = vl + vr - (2.0 * vb)
    dv = vb - (0.6 * (vb * ((vb) ** 2))) - ww + 0.5 * lap
    vn = vb + 0.4 * dv
    wn = ww + 0.5 * (f64(eps) * vn - (0.6 * ww))
    hid = f64(unit) * (vn - wn[:, unstriped(lft)])
    return mxq(f64(w3), 0, "e4m3").T @ mxq(hid, 0, "e4m3")

@@ -1,0 +1,217 @@
+import math
+from contextlib import ExitStack
+
+import concourse.mybir as mybir
+
+K, T, S, N, H = 512, 1024, 512, 256, 512
+P = 128
+PACK = 4
+FLOPS = 2 * K * H * S * 2 + 2 * H * N * S
+
+F32 = mybir.dt.float32
+BF16 = mybir.dt.bfloat16
+I32 = mybir.dt.int32
+U32 = mybir.dt.uint32
+U16 = mybir.dt.uint16
+U8 = mybir.dt.uint8
+FP8X4 = mybir.dt.float8_e4m3fn_x4
+ACT = mybir.ActivationFunctionType
+ALU = mybir.AluOpType
+
+LEFT_ON_SCALAR = (0, 1, 2, 3)
+WIDTHS = (256, 128, 128)
+V_SHARE = 44
+
+
+def tile_picked_yfhnag_two_p_kernel(
+    tc, x_words, x_scales, w1, w2, eps, unit, w3, offs, lft, rgt, out
+):
+    nc = tc.nc
+    with ExitStack() as ctx:
+        keep = ctx.enter_context(tc.tile_pool(name="keep", bufs=1))
+        psum = ctx.enter_context(tc.psum_pool(name="psum", bufs=1))
+
+        def sb(name, shape, dtype):
+            return keep.tile(shape, dtype, name=name, align_bytes=64)
+
+        offs_t = sb("offs_t", [P, S // 16], U16)
+        lft_t = sb("lft_t", [P, S // 16], U16)
+        rgt_t = sb("rgt_t", [P, S // 16], U16)
+        xw_all = sb("xw_all", [P, T], I32)
+        xs_all = sb("xs_all", [P, T], U8)
+        half = H // 2
+        w1_raw = [sb("w1_raw%d" % h, [P, PACK * half], F32) for h in range(2)]
+        w2_raw = [sb("w2_raw%d" % h, [P, PACK * half], F32) for h in range(2)]
+        w3_raw = sb("w3_raw", [P, PACK * N], F32)
+        eps_t = sb("eps_t", [P, PACK], F32)
+        unit_t = sb("unit_t", [P, PACK], F32)
+
+        def load_half(dst, w, h):
+            nc.sync.dma_start(
+                out=dst[:].rearrange("p (j c) -> p j c", j=PACK),
+                in_=w.rearrange("(p j) c -> p j c", j=PACK)[:, :, h * half : (h + 1) * half],
+            )
+
+        nc.gpsimd.memset(xs_all[:].bitcast(I32), 0)
+        nc.sync.dma_start(offs_t[:], offs)
+        nc.sync.dma_start(out=xw_all[:], in_=x_words[0].rearrange("p c r -> p (c r)").bitcast(I32))
+        for q in range(4):
+            nc.sync.dma_start(
+                out=xs_all[32 * q : 32 * q + 4, :].bitcast(I32),
+                in_=x_scales[0, 4 * q : 4 * q + 4, :].bitcast(I32),
+            )
+        for h in range(2):
+            load_half(w1_raw[h], w1, h)
+        for h in range(2):
+            load_half(w2_raw[h], w2, h)
+        nc.sync.dma_start(lft_t[:], lft)
+        nc.sync.dma_start(rgt_t[:], rgt)
+        nc.sync.dma_start(out=eps_t[:], in_=eps.rearrange("(p t) o -> p (t o)", t=PACK))
+        nc.sync.dma_start(out=unit_t[:], in_=unit.rearrange("(p t) o -> p (t o)", t=PACK))
+        nc.sync.dma_start(
+            out=w3_raw[:], in_=w3.rearrange("(p j) c -> p (j c)", j=PACK)
+        )
+
+        xw = sb("xw", [P, S], U32)
+        xs = sb("xs", [P, S], U8)
+        nc.vector.tensor_copy(xw[:], xw_all[:].bitcast(U32).indirect(offs_t[:]))
+        nc.vector.tensor_copy(xs[:], xs_all[:].indirect(offs_t[:]))
+
+        def deal(engine, grouped, raw, h, m0=0, m1=64):
+            dst = grouped[:].rearrange("p (t m j) -> p m j t", t=PACK, j=PACK)[:, 64 * h + m0 : 64 * h + m1]
+            src = raw[:].rearrange("p (j m t) -> p m j t", j=PACK, t=PACK)[:, m0:m1]
+            if engine == "scalar":
+                nc.scalar.activation(dst, src, ACT.Copy)
+            else:
+                nc.vector.tensor_copy(dst, src)
+
+        def quantize(codes, scales, grouped, c0, c1):
+            nc.vector.quantize_mx(
+                out=codes[:, c0:c1].bitcast(FP8X4),
+                scales=scales[:, c0:c1],
+                in_=grouped[:, PACK * c0 : PACK * c1],
+            )
+
+        w1_g = sb("w1_g", [P, PACK * H], BF16)
+        w2_g = sb("w2_g", [P, PACK * H], BF16)
+        w3_g = sb("w3_g", [P, PACK * N], BF16)
+        w1_q, w1_s = sb("w1_q", [P, H], U32), sb("w1_s", [P, H], U8)
+        w2_q, w2_s = sb("w2_q", [P, H], U32), sb("w2_s", [P, H], U8)
+        w3_q, w3_s = sb("w3_q", [P, N], U32), sb("w3_s", [P, N], U8)
+
+        deal("scalar", w1_g, w1_raw[0], 0)
+        deal("vector", w1_g, w1_raw[1], 1, 0, V_SHARE)
+        deal("scalar", w1_g, w1_raw[1], 1, V_SHARE, 64)
+        quantize(w1_q, w1_s, w1_g, 0, P)
+        quantize(w1_q, w1_s, w1_g, P, H)
+
+        def product(acc, codes, scales, c0, rhs, rhs_scale):
+            nc.tensor.matmul_mx(
+                out=acc,
+                lhsT=codes[:, c0 : c0 + P].bitcast(FP8X4),
+                lhsT_scale=scales[:, c0 : c0 + P],
+                rhs=rhs.bitcast(FP8X4),
+                rhs_scale=rhs_scale,
+                start=True,
+                stop=True,
+            )
+
+        c_y = sb("c_y", [P, PACK], F32)
+        c_v = sb("c_v", [P, PACK], F32)
+        c_z = sb("c_z", [P, PACK], F32)
+        nc.gpsimd.tensor_scalar(c_y[:], unit_t[:], -0.4, 0.0, ALU.mult, ALU.add)
+        nc.gpsimd.tensor_scalar(c_v[:], unit_t[:], 0.2, 0.0, ALU.mult, ALU.add)
+        nc.gpsimd.tensor_scalar(c_z[:], eps_t[:], -1.0 / 3.5, 0.0, ALU.mult, ALU.add)
+
+        vn_all = sb("vn_all", [P, PACK * S], F32)
+        g_all = sb("g_all", [P, PACK * S], F32)
+        vwin = [sb("vwin%d" % t, [P, 2 * S], F32) for t in range(PACK)]
+        zwin = [sb("zwin%d" % t, [P, 2 * S], F32) for t in range(PACK)]
+
+        def voltage(t):
+            vv = psum.tile([P, S], F32, name="vv", bufs=2)
+            product(vv[:], w1_q, w1_s, t * P, xw[:], xs[:])
+            nc.scalar.activation(vwin[t][:, :S], vv[:], ACT.Tanh)
+            nc.scalar.activation(vwin[t][:, S:], vwin[t][:, :S], ACT.Square, scale=math.sqrt(1.2))
+
+        def recovery(t):
+            ww = psum.tile([P, S], F32, name="ww", bufs=2)
+            product(ww[:], w2_q, w2_s, t * P, xw[:], xs[:])
+            nc.scalar.activation(zwin[t][:, S:], ww[:], ACT.Copy, scale=c_y[:, t : t + 1])
+
+        def left(t):
+            vl = sb("vl%d" % t, [P, S], F32)
+            nc.scalar.activation(vl[:], vwin[t][:].indirect(lft_t[:]), ACT.Copy)
+            return vl
+
+        def step(t, vl):
+            negp = sb("negp%d" % t, [P, S], F32)
+            a = sb("a%d" % t, [P, S], F32)
+            b = sb("b%d" % t, [P, S], F32)
+            nc.vector.scalar_tensor_tensor(
+                negp[:], vwin[t][:, S:], 5.0, vwin[t][:, :S], ALU.subtract, ALU.mult
+            )
+            nc.vector.tensor_tensor(a[:], vwin[t][:].indirect(rgt_t[:]), negp[:], ALU.subtract)
+            if vl is not None:
+                nc.vector.tensor_tensor(b[:], vl[:], a[:], ALU.add)
+            else:
+                nc.vector.tensor_tensor(b[:], vwin[t][:].indirect(lft_t[:]), a[:], ALU.add)
+            vn = vn_all[:, t * S : (t + 1) * S]
+            nc.vector.scalar_tensor_tensor(
+                vn, b[:], c_v[:, t : t + 1], zwin[t][:, S:], ALU.mult, ALU.add
+            )
+            nc.vector.scalar_tensor_tensor(
+                zwin[t][:, :S], vn, c_z[:, t : t + 1], zwin[t][:, S:], ALU.mult, ALU.add
+            )
+
+        def fetch(t, j0, width):
+            nc.scalar.activation(
+                g_all[:, t * S + j0 : t * S + j0 + width],
+                zwin[t][:].indirect(lft_t[:, j0 // 16 : (j0 + width) // 16]),
+                ACT.Copy,
+                scale=1.75,
+            )
+
+        for h in range(2):
+            deal("vector", w2_g, w2_raw[h], h)
+        quantize(w2_q, w2_s, w2_g, 0, H)
+        for t in range(PACK):
+            voltage(t)
+            vl = left(t) if t in LEFT_ON_SCALAR else None
+            recovery(t)
+            step(t, vl)
+        nc.scalar.activation(
+            w3_g[:].rearrange("p (c i j) -> p c j i", i=4, j=PACK),
+            w3_raw[:].rearrange("p (j c i) -> p c j i", i=4, j=PACK),
+            ACT.Copy,
+        )
+        quantize(w3_q, w3_s, w3_g, 0, N)
+        for t in range(PACK - 1):
+            fetch(t, 0, S)
+        starts = [sum(WIDTHS[:k]) for k in range(len(WIDTHS))]
+        for j0, width in zip(starts, WIDTHS):
+            fetch(PACK - 1, j0, width)
+
+        hid_g = sb("hid_g", [P, PACK * S], BF16)
+        hid_q, hid_s = sb("hid_q", [P, S], U32), sb("hid_s", [P, S], U8)
+        for part, (j0, width) in enumerate(zip(starts, WIDTHS)):
+            cols = slice(j0 // 4, (j0 + width) // 4)
+            nc.vector.tensor_tensor(
+                hid_g[:].rearrange("p (c i t) -> p c t i", i=4, t=PACK)[:, cols],
+                g_all[:].rearrange("p (t c i) -> p c t i", i=4, t=PACK)[:, cols],
+                vn_all[:].rearrange("p (t c i) -> p c t i", i=4, t=PACK)[:, cols],
+                ALU.add,
+            )
+            quantize(hid_q, hid_s, hid_g, j0, j0 + width)
+            res = sb("res%d" % part, [P, 2 * width], F32)
+            for mb in range(N // P):
+                acc = psum.tile([P, width], F32, name="acc", bufs=4)
+                product(acc[:], w3_q, w3_s, mb * P, hid_q[:, j0 : j0 + width], hid_s[:, j0 : j0 + width])
+                if mb == 0:
+                    nc.scalar.activation(res[:, :width], acc[:], ACT.Copy)
+                else:
+                    nc.vector.tensor_copy(res[:, width:], acc[:])
+            nc.sync.dma_start(
+                out=out.rearrange("(b p) j -> p b j", p=P)[:, :, j0 : j0 + width],
+                in_=res[:].rearrange("p (b j) -> p b j", b=2),
+            )

@@ -52,7 +52,7 @@ def tile_picked_yfhnag_two_p_kernel(
                 in_=w.rearrange("(p j) c -> p j c", j=PACK)[:, :, h * half : (h + 1) * half],
             )
 
-        nc.gpsimd.memset(xs_all[:].bitcast(I32), 0)
+        nc.vector.memset(xs_all[:].bitcast(I32), 0)
         nc.sync.dma_start(offs_t[:], offs)
         nc.sync.dma_start(out=xw_all[:], in_=x_words[0].rearrange("p c r -> p (c r)").bitcast(I32))
         for q in range(4):
@@ -62,15 +62,15 @@ def tile_picked_yfhnag_two_p_kernel(
             )
         for h in range(2):
             load_half(w1_raw[h], w1, h)
+        nc.sync.dma_start(rgt_t[:], rgt)
         for h in range(2):
             load_half(w2_raw[h], w2, h)
         nc.sync.dma_start(lft_t[:], lft)
-        nc.sync.dma_start(rgt_t[:], rgt)
-        nc.sync.dma_start(out=eps_t[:], in_=eps.rearrange("(p t) o -> p (t o)", t=PACK))
-        nc.sync.dma_start(out=unit_t[:], in_=unit.rearrange("(p t) o -> p (t o)", t=PACK))
         nc.sync.dma_start(
             out=w3_raw[:], in_=w3.rearrange("(p j) c -> p (j c)", j=PACK)
         )
+        nc.gpsimd.dma_start(out=eps_t[:], in_=eps.rearrange("(p t) o -> p (t o)", t=PACK))
+        nc.gpsimd.dma_start(out=unit_t[:], in_=unit.rearrange("(p t) o -> p (t o)", t=PACK))
 
         xw = sb("xw", [P, S], U32)
         xs = sb("xs", [P, S], U8)
@@ -92,8 +92,7 @@ def tile_picked_yfhnag_two_p_kernel(
                 in_=grouped[:, PACK * c0 : PACK * c1],
             )
 
-        w1_g = sb("w1_g", [P, PACK * H], BF16)
-        w2_g = sb("w2_g", [P, PACK * H], BF16)
+        w1_g = sb("w_g", [P, PACK * H], BF16)
         w3_g = sb("w3_g", [P, PACK * N], BF16)
         w1_q, w1_s = sb("w1_q", [P, H], U32), sb("w1_s", [P, H], U8)
         w2_q, w2_s = sb("w2_q", [P, H], U32), sb("w2_s", [P, H], U8)
@@ -144,25 +143,30 @@ def tile_picked_yfhnag_two_p_kernel(
             nc.scalar.activation(vl[:], vwin[t][:].indirect(lft_t[:]), ACT.Copy)
             return vl
 
-        def step(t, vl):
-            negp = sb("negp%d" % t, [P, S], F32)
-            a = sb("a%d" % t, [P, S], F32)
-            b = sb("b%d" % t, [P, S], F32)
-            nc.vector.scalar_tensor_tensor(
-                negp[:], vwin[t][:, S:], 5.0, vwin[t][:, :S], ALU.subtract, ALU.mult
-            )
-            nc.vector.tensor_tensor(a[:], vwin[t][:].indirect(rgt_t[:]), negp[:], ALU.subtract)
-            if vl is not None:
-                nc.vector.tensor_tensor(b[:], vl[:], a[:], ALU.add)
-            else:
-                nc.vector.tensor_tensor(b[:], vwin[t][:].indirect(lft_t[:]), a[:], ALU.add)
-            vn = vn_all[:, t * S : (t + 1) * S]
-            nc.vector.scalar_tensor_tensor(
-                vn, b[:], c_v[:, t : t + 1], zwin[t][:, S:], ALU.mult, ALU.add
-            )
-            nc.vector.scalar_tensor_tensor(
-                zwin[t][:, :S], vn, c_z[:, t : t + 1], zwin[t][:, S:], ALU.mult, ALU.add
-            )
+        def step(pair, vl):
+            negp = {t: sb("negp%d" % t, [P, S], F32) for t in pair}
+            a = {t: sb("a%d" % t, [P, S], F32) for t in pair}
+            b = {t: sb("b%d" % t, [P, S], F32) for t in pair}
+            vn = {t: vn_all[:, t * S : (t + 1) * S] for t in pair}
+            for t in pair:
+                nc.vector.scalar_tensor_tensor(
+                    negp[t][:], vwin[t][:, S:], 5.0, vwin[t][:, :S], ALU.subtract, ALU.mult
+                )
+            for t in pair:
+                nc.vector.tensor_tensor(a[t][:], vwin[t][:].indirect(rgt_t[:]), negp[t][:], ALU.subtract)
+            for t in pair:
+                if vl[t] is not None:
+                    nc.vector.tensor_tensor(b[t][:], vl[t][:], a[t][:], ALU.add)
+                else:
+                    nc.vector.tensor_tensor(b[t][:], vwin[t][:].indirect(lft_t[:]), a[t][:], ALU.add)
+            for t in pair:
+                nc.vector.scalar_tensor_tensor(
+                    vn[t], b[t][:], c_v[:, t : t + 1], zwin[t][:, S:], ALU.mult, ALU.add
+                )
+            for t in pair:
+                nc.vector.scalar_tensor_tensor(
+                    zwin[t][:, :S], vn[t], c_z[:, t : t + 1], zwin[t][:, S:], ALU.mult, ALU.add
+                )
 
         def fetch(t, j0, width):
             nc.scalar.activation(
@@ -172,25 +176,29 @@ def tile_picked_yfhnag_two_p_kernel(
                 scale=1.75,
             )
 
+        w2_g = sb("w_g", [P, PACK * H], BF16)
         for h in range(2):
             deal("vector", w2_g, w2_raw[h], h)
         quantize(w2_q, w2_s, w2_g, 0, H)
-        for t in range(PACK):
-            voltage(t)
-            vl = left(t) if t in LEFT_ON_SCALAR else None
-            recovery(t)
-            step(t, vl)
+        for pair in ((0, 1), (2, 3)):
+            for t in pair:
+                voltage(t)
+            vl = {t: left(t) if t in LEFT_ON_SCALAR else None for t in pair}
+            for t in pair:
+                recovery(t)
+            step(pair, vl)
         nc.scalar.activation(
             w3_g[:].rearrange("p (c i j) -> p c j i", i=4, j=PACK),
             w3_raw[:].rearrange("p (j c i) -> p c j i", i=4, j=PACK),
             ACT.Copy,
         )
         quantize(w3_q, w3_s, w3_g, 0, N)
-        for t in range(PACK - 1):
+        for t in (0, 1):
             fetch(t, 0, S)
         starts = [sum(WIDTHS[:k]) for k in range(len(WIDTHS))]
         for j0, width in zip(starts, WIDTHS):
-            fetch(PACK - 1, j0, width)
+            for t in (2, 3):
+                fetch(t, j0, width)
 
         hid_g = sb("hid_g", [P, PACK * S], BF16)
         hid_q, hid_s = sb("hid_q", [P, S], U32), sb("hid_s", [P, S], U8)
@@ -204,13 +212,10 @@ def tile_picked_yfhnag_two_p_kernel(
             )
             quantize(hid_q, hid_s, hid_g, j0, j0 + width)
             res = sb("res%d" % part, [P, 2 * width], F32)
+            acc = psum.tile([P, 2 * width], F32, name="acc", bufs=3)
             for mb in range(N // P):
-                acc = psum.tile([P, width], F32, name="acc", bufs=4)
-                product(acc[:], w3_q, w3_s, mb * P, hid_q[:, j0 : j0 + width], hid_s[:, j0 : j0 + width])
-                if mb == 0:
-                    nc.scalar.activation(res[:, :width], acc[:], ACT.Copy)
-                else:
-                    nc.vector.tensor_copy(res[:, width:], acc[:])
+                product(acc[:, mb * width : (mb + 1) * width], w3_q, w3_s, mb * P, hid_q[:, j0 : j0 + width], hid_s[:, j0 : j0 + width])
+            nc.scalar.activation(res[:], acc[:], ACT.Copy)
             nc.sync.dma_start(
                 out=out.rearrange("(b p) j -> p b j", p=P)[:, :, j0 : j0 + width],
                 in_=res[:].rearrange("p (b j) -> p b j", b=2),

@@ -187,10 +187,9 @@ def tile_picked_yfhnag_two_p_kernel(
             for t in pair:
                 recovery(t)
             step(pair, vl)
-        nc.scalar.activation(
+        nc.vector.tensor_copy(
             w3_g[:].rearrange("p (c i j) -> p c j i", i=4, j=PACK),
             w3_raw[:].rearrange("p (j c i) -> p c j i", i=4, j=PACK),
-            ACT.Copy,
         )
         quantize(w3_q, w3_s, w3_g, 0, N)
         for t in (0, 1):
@@ -212,10 +211,19 @@ def tile_picked_yfhnag_two_p_kernel(
             )
             quantize(hid_q, hid_s, hid_g, j0, j0 + width)
             res = sb("res%d" % part, [P, 2 * width], F32)
-            acc = psum.tile([P, 2 * width], F32, name="acc", bufs=3)
-            for mb in range(N // P):
-                product(acc[:, mb * width : (mb + 1) * width], w3_q, w3_s, mb * P, hid_q[:, j0 : j0 + width], hid_s[:, j0 : j0 + width])
-            nc.scalar.activation(res[:], acc[:], ACT.Copy)
+            rhs = (hid_q[:, j0 : j0 + width], hid_s[:, j0 : j0 + width])
+            if part < len(WIDTHS) - 1:
+                acc = psum.tile([P, 2 * width], F32, name="acc", bufs=4)
+                for mb in range(N // P):
+                    product(acc[:, mb * width : (mb + 1) * width], w3_q, w3_s, mb * P, *rhs)
+                nc.scalar.activation(res[:], acc[:], ACT.Copy)
+            else:
+                acc = psum.tile([P, width], F32, name="acc", bufs=4)
+                product(acc[:], w3_q, w3_s, 0, *rhs)
+                nc.scalar.activation(res[:, :width], acc[:], ACT.Copy)
+                acc = psum.tile([P, width], F32, name="acc", bufs=4)
+                product(acc[:], w3_q, w3_s, P, *rhs)
+                nc.vector.tensor_copy(res[:, width:], acc[:])
             nc.sync.dma_start(
                 out=out.rearrange("(b p) j -> p b j", p=P)[:, :, j0 : j0 + width],
                 in_=res[:].rearrange("p (b j) -> p b j", b=2),

@@ -4,9 +4,17 @@ from contextlib import ExitStack
 import concourse.mybir as mybir
 
 K, T, S, N, H = 512, 1024, 512, 256, 512
+FLOPS = 2 * (2 * K * H * S) + 2 * H * N * S
+
 P = 128
 PACK = 4
-FLOPS = 2 * K * H * S * 2 + 2 * H * N * S
+LIST_ROWS = 16
+HALF_H = H // 2
+HALF_M = HALF_H // PACK
+HALF_S = S // 2
+PAIRS = ((0, 1), (2, 3))
+PART_WIDTHS = (256, 128, 128)
+VECTOR_SHARE = 44
 
 F32 = mybir.dt.float32
 BF16 = mybir.dt.bfloat16
@@ -17,10 +25,6 @@ U8 = mybir.dt.uint8
 FP8X4 = mybir.dt.float8_e4m3fn_x4
 ACT = mybir.ActivationFunctionType
 ALU = mybir.AluOpType
-
-LEFT_ON_SCALAR = (0, 1, 2, 3)
-WIDTHS = (256, 128, 128)
-V_SHARE = 44
 
 
 def tile_picked_yfhnag_two_p_kernel(
@@ -34,27 +38,26 @@ def tile_picked_yfhnag_two_p_kernel(
         def sb(name, shape, dtype):
             return keep.tile(shape, dtype, name=name, align_bytes=64)
 
-        offs_t = sb("offs_t", [P, S // 16], U16)
-        lft_t = sb("lft_t", [P, S // 16], U16)
-        rgt_t = sb("rgt_t", [P, S // 16], U16)
+        offs_t = sb("offs_t", [P, S // LIST_ROWS], U16)
+        lft_t = sb("lft_t", [P, S // LIST_ROWS], U16)
+        rgt_t = sb("rgt_t", [P, S // LIST_ROWS], U16)
         xw_all = sb("xw_all", [P, T], I32)
         xs_all = sb("xs_all", [P, T], U8)
-        half = H // 2
-        w1_raw = [sb("w1_raw%d" % h, [P, PACK * half], F32) for h in range(2)]
-        w2_raw = [sb("w2_raw%d" % h, [P, PACK * half], F32) for h in range(2)]
+        w1_raw = [sb("w1_raw%d" % h, [P, PACK * HALF_H], F32) for h in range(2)]
+        w2_raw = [sb("w2_raw%d" % h, [P, PACK * HALF_H], F32) for h in range(2)]
         w3_raw = sb("w3_raw", [P, PACK * N], F32)
         eps_t = sb("eps_t", [P, PACK], F32)
         unit_t = sb("unit_t", [P, PACK], F32)
 
-        def load_half(dst, w, h):
+        def load_half(raw, w, h):
             nc.sync.dma_start(
-                out=dst[:].rearrange("p (j c) -> p j c", j=PACK),
-                in_=w.rearrange("(p j) c -> p j c", j=PACK)[:, :, h * half : (h + 1) * half],
+                out=raw[:].rearrange("p (j c) -> p j c", j=PACK),
+                in_=w.rearrange("(p j) c -> p j c", j=PACK)[:, :, h * HALF_H : (h + 1) * HALF_H],
             )
 
         nc.vector.memset(xs_all[:].bitcast(I32), 0)
-        nc.sync.dma_start(offs_t[:], offs)
         nc.sync.dma_start(out=xw_all[:], in_=x_words[0].rearrange("p c r -> p (c r)").bitcast(I32))
+        nc.sync.dma_start(offs_t[:], offs)
         for q in range(4):
             nc.sync.dma_start(
                 out=xs_all[32 * q : 32 * q + 4, :].bitcast(I32),
@@ -66,9 +69,7 @@ def tile_picked_yfhnag_two_p_kernel(
         for h in range(2):
             load_half(w2_raw[h], w2, h)
         nc.sync.dma_start(lft_t[:], lft)
-        nc.sync.dma_start(
-            out=w3_raw[:], in_=w3.rearrange("(p j) c -> p (j c)", j=PACK)
-        )
+        nc.sync.dma_start(out=w3_raw[:], in_=w3.rearrange("(p j) c -> p (j c)", j=PACK))
         nc.gpsimd.dma_start(out=eps_t[:], in_=eps.rearrange("(p t) o -> p (t o)", t=PACK))
         nc.gpsimd.dma_start(out=unit_t[:], in_=unit.rearrange("(p t) o -> p (t o)", t=PACK))
 
@@ -77,32 +78,13 @@ def tile_picked_yfhnag_two_p_kernel(
         nc.vector.tensor_copy(xw[:], xw_all[:].bitcast(U32).indirect(offs_t[:]))
         nc.vector.tensor_copy(xs[:], xs_all[:].indirect(offs_t[:]))
 
-        def deal(engine, grouped, raw, h, m0=0, m1=64):
-            dst = grouped[:].rearrange("p (t m j) -> p m j t", t=PACK, j=PACK)[:, 64 * h + m0 : 64 * h + m1]
-            src = raw[:].rearrange("p (j m t) -> p m j t", j=PACK, t=PACK)[:, m0:m1]
-            if engine == "scalar":
-                nc.scalar.activation(dst, src, ACT.Copy)
-            else:
-                nc.vector.tensor_copy(dst, src)
+        def dealt_views(grouped, raw, h, m0, m1):
+            dst = grouped[:].rearrange("p (t m j) -> p m j t", t=PACK, j=PACK)
+            src = raw[:].rearrange("p (j m t) -> p m j t", j=PACK, t=PACK)
+            return dst[:, HALF_M * h + m0 : HALF_M * h + m1], src[:, m0:m1]
 
-        def quantize(codes, scales, grouped, c0, c1):
-            nc.vector.quantize_mx(
-                out=codes[:, c0:c1].bitcast(FP8X4),
-                scales=scales[:, c0:c1],
-                in_=grouped[:, PACK * c0 : PACK * c1],
-            )
-
-        w1_g = sb("w_g", [P, PACK * H], BF16)
-        w3_g = sb("w3_g", [P, PACK * N], BF16)
-        w1_q, w1_s = sb("w1_q", [P, H], U32), sb("w1_s", [P, H], U8)
-        w2_q, w2_s = sb("w2_q", [P, H], U32), sb("w2_s", [P, H], U8)
-        w3_q, w3_s = sb("w3_q", [P, N], U32), sb("w3_s", [P, N], U8)
-
-        deal("scalar", w1_g, w1_raw[0], 0)
-        deal("vector", w1_g, w1_raw[1], 1, 0, V_SHARE)
-        deal("scalar", w1_g, w1_raw[1], 1, V_SHARE, 64)
-        quantize(w1_q, w1_s, w1_g, 0, P)
-        quantize(w1_q, w1_s, w1_g, P, H)
+        def quantize(codes, scales, values):
+            nc.vector.quantize_mx(out=codes.bitcast(FP8X4), scales=scales, in_=values)
 
         def product(acc, codes, scales, c0, rhs, rhs_scale):
             nc.tensor.matmul_mx(
@@ -115,107 +97,123 @@ def tile_picked_yfhnag_two_p_kernel(
                 stop=True,
             )
 
-        c_y = sb("c_y", [P, PACK], F32)
-        c_v = sb("c_v", [P, PACK], F32)
-        c_z = sb("c_z", [P, PACK], F32)
-        nc.gpsimd.tensor_scalar(c_y[:], unit_t[:], -0.4, 0.0, ALU.mult, ALU.add)
-        nc.gpsimd.tensor_scalar(c_v[:], unit_t[:], 0.2, 0.0, ALU.mult, ALU.add)
-        nc.gpsimd.tensor_scalar(c_z[:], eps_t[:], -1.0 / 3.5, 0.0, ALU.mult, ALU.add)
+        w1_g = sb("w_grouped", [P, PACK * H], BF16)
+        w3_g = sb("w3_grouped", [P, PACK * N], BF16)
+        w1_q, w1_s = sb("w1_q", [P, H], U32), sb("w1_s", [P, H], U8)
+        w2_q, w2_s = sb("w2_q", [P, H], U32), sb("w2_s", [P, H], U8)
+        w3_q, w3_s = sb("w3_q", [P, N], U32), sb("w3_s", [P, N], U8)
 
-        vn_all = sb("vn_all", [P, PACK * S], F32)
-        g_all = sb("g_all", [P, PACK * S], F32)
-        vwin = [sb("vwin%d" % t, [P, 2 * S], F32) for t in range(PACK)]
-        zwin = [sb("zwin%d" % t, [P, 2 * S], F32) for t in range(PACK)]
+        nc.scalar.activation(*dealt_views(w1_g, w1_raw[0], 0, 0, HALF_M), ACT.Copy)
+        nc.vector.tensor_copy(*dealt_views(w1_g, w1_raw[1], 1, 0, VECTOR_SHARE))
+        nc.scalar.activation(*dealt_views(w1_g, w1_raw[1], 1, VECTOR_SHARE, HALF_M), ACT.Copy)
+        quantize(w1_q[:, :P], w1_s[:, :P], w1_g[:, : PACK * P])
+        quantize(w1_q[:, P:], w1_s[:, P:], w1_g[:, PACK * P :])
+
+        c_drive = sb("c_drive", [P, PACK], F32)
+        c_volt = sb("c_volt", [P, PACK], F32)
+        c_recov = sb("c_recov", [P, PACK], F32)
+        nc.gpsimd.tensor_scalar(c_drive[:], unit_t[:], -0.4, 0.0, ALU.mult, ALU.add)
+        nc.gpsimd.tensor_scalar(c_volt[:], unit_t[:], 0.2, 0.0, ALU.mult, ALU.add)
+        nc.gpsimd.tensor_scalar(c_recov[:], eps_t[:], -1.0 / 3.5, 0.0, ALU.mult, ALU.add)
+
+        volt_all = sb("volt_all", [P, PACK * S], F32)
+        fetched = [sb("fetched%d" % h, [P, PACK * HALF_S], F32) for h in range(2)]
+        vb_sq = [sb("vb_sq%d" % t, [P, 2 * S], F32) for t in range(PACK)]
+        recov = [sb("recov%d" % t, [P, S], F32) for t in range(PACK)]
+        drive = [sb("drive%d" % t, [P, S], F32)[:] for t in range(PACK - 1)]
+        drive.append(fetched[1][:, 2 * HALF_S :])
 
         def voltage(t):
             vv = psum.tile([P, S], F32, name="vv", bufs=2)
             product(vv[:], w1_q, w1_s, t * P, xw[:], xs[:])
-            nc.scalar.activation(vwin[t][:, :S], vv[:], ACT.Tanh)
-            nc.scalar.activation(vwin[t][:, S:], vwin[t][:, :S], ACT.Square, scale=math.sqrt(1.2))
+            nc.scalar.activation(vb_sq[t][:, :S], vv[:], ACT.Tanh)
+            nc.scalar.activation(vb_sq[t][:, S:], vb_sq[t][:, :S], ACT.Square, scale=math.sqrt(1.2))
 
-        def recovery(t):
-            ww = psum.tile([P, S], F32, name="ww", bufs=2)
-            product(ww[:], w2_q, w2_s, t * P, xw[:], xs[:])
-            nc.scalar.activation(zwin[t][:, S:], ww[:], ACT.Copy, scale=c_y[:, t : t + 1])
-
-        def left(t):
+        def left_neighbours(t):
             vl = sb("vl%d" % t, [P, S], F32)
-            nc.scalar.activation(vl[:], vwin[t][:].indirect(lft_t[:]), ACT.Copy)
+            nc.scalar.activation(vl[:], vb_sq[t][:].indirect(lft_t[:]), ACT.Copy)
             return vl
 
+        def recovery_drive(t):
+            ww = psum.tile([P, S], F32, name="ww", bufs=2)
+            product(ww[:], w2_q, w2_s, t * P, xw[:], xs[:])
+            nc.scalar.activation(drive[t], ww[:], ACT.Copy, scale=c_drive[:, t : t + 1])
+
         def step(pair, vl):
-            negp = {t: sb("negp%d" % t, [P, S], F32) for t in pair}
-            a = {t: sb("a%d" % t, [P, S], F32) for t in pair}
-            b = {t: sb("b%d" % t, [P, S], F32) for t in pair}
-            vn = {t: vn_all[:, t * S : (t + 1) * S] for t in pair}
+            cubic = {t: sb("cubic%d" % t, [P, S], F32) for t in pair}
+            partial = {t: sb("partial%d" % t, [P, S], F32) for t in pair}
+            total = {t: sb("total%d" % t, [P, S], F32) for t in pair}
+            volt = {t: volt_all[:, t * S : (t + 1) * S] for t in pair}
             for t in pair:
                 nc.vector.scalar_tensor_tensor(
-                    negp[t][:], vwin[t][:, S:], 5.0, vwin[t][:, :S], ALU.subtract, ALU.mult
+                    cubic[t][:], vb_sq[t][:, S:], 5.0, vb_sq[t][:, :S], ALU.subtract, ALU.mult
                 )
             for t in pair:
-                nc.vector.tensor_tensor(a[t][:], vwin[t][:].indirect(rgt_t[:]), negp[t][:], ALU.subtract)
+                nc.vector.tensor_tensor(
+                    partial[t][:], vb_sq[t][:].indirect(rgt_t[:]), cubic[t][:], ALU.subtract
+                )
             for t in pair:
-                if vl[t] is not None:
-                    nc.vector.tensor_tensor(b[t][:], vl[t][:], a[t][:], ALU.add)
-                else:
-                    nc.vector.tensor_tensor(b[t][:], vwin[t][:].indirect(lft_t[:]), a[t][:], ALU.add)
+                nc.vector.tensor_tensor(total[t][:], vl[t][:], partial[t][:], ALU.add)
             for t in pair:
                 nc.vector.scalar_tensor_tensor(
-                    vn[t], b[t][:], c_v[:, t : t + 1], zwin[t][:, S:], ALU.mult, ALU.add
+                    volt[t], total[t][:], c_volt[:, t : t + 1], drive[t], ALU.mult, ALU.add
                 )
             for t in pair:
                 nc.vector.scalar_tensor_tensor(
-                    zwin[t][:, :S], vn[t], c_z[:, t : t + 1], zwin[t][:, S:], ALU.mult, ALU.add
+                    recov[t][:], volt[t], c_recov[:, t : t + 1], drive[t], ALU.mult, ALU.add
                 )
 
-        def fetch(t, j0, width):
+        def fetch(t, h):
+            entries = lft_t[:, h * HALF_S // LIST_ROWS : (h + 1) * HALF_S // LIST_ROWS]
             nc.scalar.activation(
-                g_all[:, t * S + j0 : t * S + j0 + width],
-                zwin[t][:].indirect(lft_t[:, j0 // 16 : (j0 + width) // 16]),
+                fetched[h][:, t * HALF_S : (t + 1) * HALF_S],
+                recov[t][:].indirect(entries),
                 ACT.Copy,
                 scale=1.75,
             )
 
-        w2_g = sb("w_g", [P, PACK * H], BF16)
+        w2_g = sb("w_grouped", [P, PACK * H], BF16)
         for h in range(2):
-            deal("vector", w2_g, w2_raw[h], h)
-        quantize(w2_q, w2_s, w2_g, 0, H)
-        for pair in ((0, 1), (2, 3)):
+            nc.vector.tensor_copy(*dealt_views(w2_g, w2_raw[h], h, 0, HALF_M))
+        quantize(w2_q[:], w2_s[:], w2_g[:])
+
+        for pair in PAIRS:
             for t in pair:
                 voltage(t)
-            vl = {t: left(t) if t in LEFT_ON_SCALAR else None for t in pair}
+            vl = {t: left_neighbours(t) for t in pair}
             for t in pair:
-                recovery(t)
+                recovery_drive(t)
             step(pair, vl)
+
         nc.vector.tensor_copy(
             w3_g[:].rearrange("p (c i j) -> p c j i", i=4, j=PACK),
             w3_raw[:].rearrange("p (j c i) -> p c j i", i=4, j=PACK),
         )
-        quantize(w3_q, w3_s, w3_g, 0, N)
-        for t in (0, 1):
-            fetch(t, 0, S)
-        starts = [sum(WIDTHS[:k]) for k in range(len(WIDTHS))]
-        for j0, width in zip(starts, WIDTHS):
-            for t in (2, 3):
-                fetch(t, j0, width)
+        quantize(w3_q[:], w3_s[:], w3_g[:])
 
-        hid_g = sb("hid_g", [P, PACK * S], BF16)
+        for pair in PAIRS:
+            for h in range(2):
+                for t in pair:
+                    fetch(t, h)
+
         hid_q, hid_s = sb("hid_q", [P, S], U32), sb("hid_s", [P, S], U8)
-        for part, (j0, width) in enumerate(zip(starts, WIDTHS)):
-            cols = slice(j0 // 4, (j0 + width) // 4)
+        for part, width in enumerate(PART_WIDTHS):
+            j0 = sum(PART_WIDTHS[:part])
+            h, c0 = divmod(j0, HALF_S)
+            hid_g = sb("hid_grouped%d" % part, [P, PACK * width], BF16)
             nc.vector.tensor_tensor(
-                hid_g[:].rearrange("p (c i t) -> p c t i", i=4, t=PACK)[:, cols],
-                g_all[:].rearrange("p (t c i) -> p c t i", i=4, t=PACK)[:, cols],
-                vn_all[:].rearrange("p (t c i) -> p c t i", i=4, t=PACK)[:, cols],
+                hid_g[:].rearrange("p (c i t) -> p c t i", i=4, t=PACK),
+                fetched[h][:].rearrange("p (t c i) -> p c t i", i=4, t=PACK)[:, c0 // 4 : (c0 + width) // 4],
+                volt_all[:].rearrange("p (t c i) -> p c t i", i=4, t=PACK)[:, j0 // 4 : (j0 + width) // 4],
                 ALU.add,
             )
-            quantize(hid_q, hid_s, hid_g, j0, j0 + width)
-            res = sb("res%d" % part, [P, 2 * width], F32)
             rhs = (hid_q[:, j0 : j0 + width], hid_s[:, j0 : j0 + width])
-            if part < len(WIDTHS) - 1:
+            quantize(*rhs, hid_g[:])
+            res = sb("res%d" % part, [P, 2 * width], F32)
+            if part < len(PART_WIDTHS) - 1:
                 acc = psum.tile([P, 2 * width], F32, name="acc", bufs=4)
-                for mb in range(N // P):
-                    product(acc[:, mb * width : (mb + 1) * width], w3_q, w3_s, mb * P, *rhs)
+                for b in range(N // P):
+                    product(acc[:, b * width : (b + 1) * width], w3_q, w3_s, b * P, *rhs)
                 nc.scalar.activation(res[:], acc[:], ACT.Copy)
             else:
                 acc = psum.tile([P, width], F32, name="acc", bufs=4)

import math
from contextlib import ExitStack

import concourse.mybir as mybir

K, T, S, N, H = 512, 1024, 512, 256, 512
FLOPS = 2 * (2 * K * H * S) + 2 * H * N * S

P = 128
PACK = 4
LIST_ROWS = 16
HALF_H = H // 2
HALF_M = HALF_H // PACK
HALF_S = S // 2
PAIRS = ((0, 1), (2, 3))
PART_WIDTHS = (256, 128, 128)
VECTOR_SHARE = 44

F32 = mybir.dt.float32
BF16 = mybir.dt.bfloat16
I32 = mybir.dt.int32
U32 = mybir.dt.uint32
U16 = mybir.dt.uint16
U8 = mybir.dt.uint8
FP8X4 = mybir.dt.float8_e4m3fn_x4
ACT = mybir.ActivationFunctionType
ALU = mybir.AluOpType


def tile_picked_yfhnag_two_p_kernel(
    tc, x_words, x_scales, w1, w2, eps, unit, w3, offs, lft, rgt, out
):
    nc = tc.nc
    with ExitStack() as ctx:
        keep = ctx.enter_context(tc.tile_pool(name="keep", bufs=1))
        psum = ctx.enter_context(tc.psum_pool(name="psum", bufs=1))

        def sb(name, shape, dtype):
            return keep.tile(shape, dtype, name=name, align_bytes=64)

        offs_t = sb("offs_t", [P, S // LIST_ROWS], U16)
        lft_t = sb("lft_t", [P, S // LIST_ROWS], U16)
        rgt_t = sb("rgt_t", [P, S // LIST_ROWS], U16)
        xw_all = sb("xw_all", [P, T], I32)
        xs_all = sb("xs_all", [P, T], U8)
        w1_raw = [sb("w1_raw%d" % h, [P, PACK * HALF_H], F32) for h in range(2)]
        w2_raw = [sb("w2_raw%d" % h, [P, PACK * HALF_H], F32) for h in range(2)]
        w3_raw = sb("w3_raw", [P, PACK * N], F32)
        eps_t = sb("eps_t", [P, PACK], F32)
        unit_t = sb("unit_t", [P, PACK], F32)

        def load_half(raw, w, h):
            nc.sync.dma_start(
                out=raw[:].rearrange("p (j c) -> p j c", j=PACK),
                in_=w.rearrange("(p j) c -> p j c", j=PACK)[:, :, h * HALF_H : (h + 1) * HALF_H],
            )

        nc.vector.memset(xs_all[:].bitcast(I32), 0)
        nc.sync.dma_start(out=xw_all[:], in_=x_words[0].rearrange("p c r -> p (c r)").bitcast(I32))
        nc.sync.dma_start(offs_t[:], offs)
        for q in range(4):
            nc.sync.dma_start(
                out=xs_all[32 * q : 32 * q + 4, :].bitcast(I32),
                in_=x_scales[0, 4 * q : 4 * q + 4, :].bitcast(I32),
            )
        for h in range(2):
            load_half(w1_raw[h], w1, h)
        nc.sync.dma_start(rgt_t[:], rgt)
        for h in range(2):
            load_half(w2_raw[h], w2, h)
        nc.sync.dma_start(lft_t[:], lft)
        nc.sync.dma_start(out=w3_raw[:], in_=w3.rearrange("(p j) c -> p (j c)", j=PACK))
        nc.gpsimd.dma_start(out=eps_t[:], in_=eps.rearrange("(p t) o -> p (t o)", t=PACK))
        nc.gpsimd.dma_start(out=unit_t[:], in_=unit.rearrange("(p t) o -> p (t o)", t=PACK))

        xw = sb("xw", [P, S], U32)
        xs = sb("xs", [P, S], U8)
        nc.vector.tensor_copy(xw[:], xw_all[:].bitcast(U32).indirect(offs_t[:]))
        nc.vector.tensor_copy(xs[:], xs_all[:].indirect(offs_t[:]))

        def dealt_views(grouped, raw, h, m0, m1):
            dst = grouped[:].rearrange("p (t m j) -> p m j t", t=PACK, j=PACK)
            src = raw[:].rearrange("p (j m t) -> p m j t", j=PACK, t=PACK)
            return dst[:, HALF_M * h + m0 : HALF_M * h + m1], src[:, m0:m1]

        def quantize(codes, scales, values):
            nc.vector.quantize_mx(out=codes.bitcast(FP8X4), scales=scales, in_=values)

        def product(acc, codes, scales, c0, rhs, rhs_scale):
            nc.tensor.matmul_mx(
                out=acc,
                lhsT=codes[:, c0 : c0 + P].bitcast(FP8X4),
                lhsT_scale=scales[:, c0 : c0 + P],
                rhs=rhs.bitcast(FP8X4),
                rhs_scale=rhs_scale,
                start=True,
                stop=True,
            )

        w1_g = sb("w_grouped", [P, PACK * H], BF16)
        w3_g = sb("w3_grouped", [P, PACK * N], BF16)
        w1_q, w1_s = sb("w1_q", [P, H], U32), sb("w1_s", [P, H], U8)
        w2_q, w2_s = sb("w2_q", [P, H], U32), sb("w2_s", [P, H], U8)
        w3_q, w3_s = sb("w3_q", [P, N], U32), sb("w3_s", [P, N], U8)

        nc.scalar.activation(*dealt_views(w1_g, w1_raw[0], 0, 0, HALF_M), ACT.Copy)
        nc.vector.tensor_copy(*dealt_views(w1_g, w1_raw[1], 1, 0, VECTOR_SHARE))
        nc.scalar.activation(*dealt_views(w1_g, w1_raw[1], 1, VECTOR_SHARE, HALF_M), ACT.Copy)
        quantize(w1_q[:, :P], w1_s[:, :P], w1_g[:, : PACK * P])
        quantize(w1_q[:, P:], w1_s[:, P:], w1_g[:, PACK * P :])

        c_drive = sb("c_drive", [P, PACK], F32)
        c_volt = sb("c_volt", [P, PACK], F32)
        c_recov = sb("c_recov", [P, PACK], F32)
        nc.gpsimd.tensor_scalar(c_drive[:], unit_t[:], -0.4, 0.0, ALU.mult, ALU.add)
        nc.gpsimd.tensor_scalar(c_volt[:], unit_t[:], 0.2, 0.0, ALU.mult, ALU.add)
        nc.gpsimd.tensor_scalar(c_recov[:], eps_t[:], -1.0 / 3.5, 0.0, ALU.mult, ALU.add)

        volt_all = sb("volt_all", [P, PACK * S], F32)
        fetched = [sb("fetched%d" % h, [P, PACK * HALF_S], F32) for h in range(2)]
        vb_sq = [sb("vb_sq%d" % t, [P, 2 * S], F32) for t in range(PACK)]
        recov = [sb("recov%d" % t, [P, S], F32) for t in range(PACK)]
        drive = [sb("drive%d" % t, [P, S], F32)[:] for t in range(PACK - 1)]
        drive.append(fetched[1][:, 2 * HALF_S :])

        def voltage(t):
            vv = psum.tile([P, S], F32, name="vv", bufs=2)
            product(vv[:], w1_q, w1_s, t * P, xw[:], xs[:])
            nc.scalar.activation(vb_sq[t][:, :S], vv[:], ACT.Tanh)
            nc.scalar.activation(vb_sq[t][:, S:], vb_sq[t][:, :S], ACT.Square, scale=math.sqrt(1.2))

        def left_neighbours(t):
            vl = sb("vl%d" % t, [P, S], F32)
            nc.scalar.activation(vl[:], vb_sq[t][:].indirect(lft_t[:]), ACT.Copy)
            return vl

        def recovery_drive(t):
            ww = psum.tile([P, S], F32, name="ww", bufs=2)
            product(ww[:], w2_q, w2_s, t * P, xw[:], xs[:])
            nc.scalar.activation(drive[t], ww[:], ACT.Copy, scale=c_drive[:, t : t + 1])

        def step(pair, vl):
            cubic = {t: sb("cubic%d" % t, [P, S], F32) for t in pair}
            partial = {t: sb("partial%d" % t, [P, S], F32) for t in pair}
            total = {t: sb("total%d" % t, [P, S], F32) for t in pair}
            volt = {t: volt_all[:, t * S : (t + 1) * S] for t in pair}
            for t in pair:
                nc.vector.scalar_tensor_tensor(
                    cubic[t][:], vb_sq[t][:, S:], 5.0, vb_sq[t][:, :S], ALU.subtract, ALU.mult
                )
            for t in pair:
                nc.vector.tensor_tensor(
                    partial[t][:], vb_sq[t][:].indirect(rgt_t[:]), cubic[t][:], ALU.subtract
                )
            for t in pair:
                nc.vector.tensor_tensor(total[t][:], vl[t][:], partial[t][:], ALU.add)
            for t in pair:
                nc.vector.scalar_tensor_tensor(
                    volt[t], total[t][:], c_volt[:, t : t + 1], drive[t], ALU.mult, ALU.add
                )
            for t in pair:
                nc.vector.scalar_tensor_tensor(
                    recov[t][:], volt[t], c_recov[:, t : t + 1], drive[t], ALU.mult, ALU.add
                )

        def fetch(t, h):
            entries = lft_t[:, h * HALF_S // LIST_ROWS : (h + 1) * HALF_S // LIST_ROWS]
            nc.scalar.activation(
                fetched[h][:, t * HALF_S : (t + 1) * HALF_S],
                recov[t][:].indirect(entries),
                ACT.Copy,
                scale=1.75,
            )

        w2_g = sb("w_grouped", [P, PACK * H], BF16)
        for h in range(2):
            nc.vector.tensor_copy(*dealt_views(w2_g, w2_raw[h], h, 0, HALF_M))
        quantize(w2_q[:], w2_s[:], w2_g[:])

        for pair in PAIRS:
            for t in pair:
                voltage(t)
            vl = {t: left_neighbours(t) for t in pair}
            for t in pair:
                recovery_drive(t)
            step(pair, vl)

        nc.vector.tensor_copy(
            w3_g[:].rearrange("p (c i j) -> p c j i", i=4, j=PACK),
            w3_raw[:].rearrange("p (j c i) -> p c j i", i=4, j=PACK),
        )
        quantize(w3_q[:], w3_s[:], w3_g[:])

        for pair in PAIRS:
            for h in range(2):
                for t in pair:
                    fetch(t, h)

        hid_q, hid_s = sb("hid_q", [P, S], U32), sb("hid_s", [P, S], U8)
        for part, width in enumerate(PART_WIDTHS):
            j0 = sum(PART_WIDTHS[:part])
            h, c0 = divmod(j0, HALF_S)
            hid_g = sb("hid_grouped%d" % part, [P, PACK * width], BF16)
            nc.vector.tensor_tensor(
                hid_g[:].rearrange("p (c i t) -> p c t i", i=4, t=PACK),
                fetched[h][:].rearrange("p (t c i) -> p c t i", i=4, t=PACK)[:, c0 // 4 : (c0 + width) // 4],
                volt_all[:].rearrange("p (t c i) -> p c t i", i=4, t=PACK)[:, j0 // 4 : (j0 + width) // 4],
                ALU.add,
            )
            rhs = (hid_q[:, j0 : j0 + width], hid_s[:, j0 : j0 + width])
            quantize(*rhs, hid_g[:])
            res = sb("res%d" % part, [P, 2 * width], F32)
            if part < len(PART_WIDTHS) - 1:
                acc = psum.tile([P, 2 * width], F32, name="acc", bufs=4)
                for b in range(N // P):
                    product(acc[:, b * width : (b + 1) * width], w3_q, w3_s, b * P, *rhs)
                nc.scalar.activation(res[:], acc[:], ACT.Copy)
            else:
                acc = psum.tile([P, width], F32, name="acc", bufs=4)
                product(acc[:], w3_q, w3_s, 0, *rhs)
                nc.scalar.activation(res[:, :width], acc[:], ACT.Copy)
                acc = psum.tile([P, width], F32, name="acc", bufs=4)
                product(acc[:], w3_q, w3_s, P, *rhs)
                nc.vector.tensor_copy(res[:, width:], acc[:])
            nc.sync.dma_start(
                out=out.rearrange("(b p) j -> p b j", p=P)[:, :, j0 : j0 + width],
                in_=res[:].rearrange("p (b j) -> p b j", b=2),
            )
